import numpy as np
import ml_dtypes


def mxq(x, axis, fmt="e4m3"):
    dtype, down = {"e4m3": (ml_dtypes.float8_e4m3fn, 7), "e5m2": (ml_dtypes.float8_e5m2, 14)}[fmt]
    v = np.moveaxis(np.asarray(x, np.float32).astype(ml_dtypes.bfloat16).astype(np.float64), axis, -1)
    blocks = v.reshape(v.shape[:-1] + (-1, 32))
    amax = np.abs(blocks).max(-1, keepdims=True)
    byte = np.maximum(np.where(amax > 0, np.frexp(amax)[1] - 1 + 127, 0) - down, 1)
    scale = np.exp2(byte - 127.0)
    codes = (blocks / scale).astype(np.float32).astype(dtype).astype(np.float64)
    return np.moveaxis((codes * scale).reshape(v.shape), -1, axis)


WIDE = False


def mx_kscale(k):
    if not WIDE:
        return np.ones(k)
    levels = np.array([30, -30])
    if k % 512:
        return np.exp2(np.random.permutation(np.resize(levels, k // 32))).repeat(32)
    a = np.empty((k // 512, 16))
    for p in range(k // 512):
        a[p, :8] = np.random.permutation(np.resize(levels, 8))
        for g in range(8):
            far = levels[np.abs(levels - a[p, g]) >= 10]
            a[p, g + 8] = far[np.random.randint(len(far))]
    return np.exp2(a.ravel()).repeat(32)


BF16 = ml_dtypes.bfloat16


def bf(x):
    return np.asarray(x, np.float32).astype(BF16)


def f64(x):
    return np.asarray(x).astype(np.float64)


E2M1 = np.array([0.0, 0.5, 1.0, 1.5, 2.0, 3.0, 4.0, 6.0, -0.0, -0.5, -1.0, -1.5, -2.0, -3.0, -4.0, -6.0])


def pack_weight(w, fmt):
    k, n = w.shape
    w = f64(bf(w)).reshape(k // 32, 32, n)
    amax = np.abs(w).max(1)
    if fmt in ("e4m3", "e5m2"):
        byte = np.frexp(amax)[1] - 1 + 127 - (7 if fmt == "e4m3" else 14)
    else:
        mant, ex = np.frexp(amax / 6.0)
        byte = np.where(mant > 0.5, ex, ex - 1) + 127
    byte = np.clip(np.where(amax > 0, byte, 1), 1, 254)
    scaled = (w * np.exp2(127.0 - byte)[:, None, :]).reshape(k, n).astype(np.float32)
    by_word = np.ascontiguousarray(scaled.reshape(k // 512, 128, 4, n).transpose(0, 1, 3, 2))
    if fmt in ("e4m3", "e5m2"):
        words = by_word.astype(ml_dtypes.float8_e4m3fn if fmt == "e4m3" else ml_dtypes.float8_e5m2).view(np.uint8)
    else:
        c = by_word.astype(ml_dtypes.float4_e2m1fn).view(np.uint8) & 0xF
        words = c[..., 0::2] | (c[..., 1::2] << 4)
    return np.ascontiguousarray(words), np.ascontiguousarray(byte.astype(np.uint8).reshape(k // 512, 16, n))


def unpack_weight(words, scales, fmt):
    g, p, n, _ = words.shape
    if fmt in ("e4m3", "e5m2"):
        vals = np.ascontiguousarray(words).view(ml_dtypes.float8_e4m3fn if fmt == "e4m3" else ml_dtypes.float8_e5m2).astype(np.float64)
    else:
        nib = np.empty((g, p, n, 4), np.uint8)
        nib[..., 0::2] = words & 0xF
        nib[..., 1::2] = words >> 4
        vals = E2M1[nib]
    vals = vals * np.repeat(np.exp2(scales.astype(np.float64) - 127.0), 8, axis=1)[..., None]
    return vals.transpose(0, 1, 3, 2).reshape(g * 512, n)

def planes(Y):
    n, m = Y.shape
    b = f64(bf(Y)).reshape(n // 32, 32, m)
    amax = np.abs(b).max(1)
    byte = np.clip(np.where(amax > 0, np.frexp(amax)[1] - 1 + 127 - 7, 1), 1, 254)
    codes = (b * np.exp2(127.0 - byte)[:, None, :]).reshape(n, m).astype(np.float32).astype(ml_dtypes.float8_e4m3fn).view(np.uint8)
    words = codes.reshape(n // 512, 128, 4, m).transpose(0, 1, 3, 2)
    return np.ascontiguousarray(words), np.ascontiguousarray(byte.astype(np.uint8).reshape(n // 512, 16, m))


FRAMES, PITCHES, BINS, HARMONICS, PER_OCTAVE = 1024, 1024, 2048, 16, 256
COMB_WIDTH = 8.0

def harmonic_combs():
    b = np.arange(BINS)[:, None]
    p = np.arange(PITCHES)[None, :]
    c = np.zeros((BINS, PITCHES))
    for h in range(1, HARMONICS + 1):
        c += h ** -0.5 * np.exp(-0.5 * ((b - p - PER_OCTAVE * np.log2(h)) / COMB_WIDTH) ** 2)
    return c

def setup_inputs():
    s = mx_kscale(PITCHES)
    P = np.exp(1.5 * np.random.randn(PITCHES, FRAMES))
    P = P / P.sum(axis=0, keepdims=True)
    D = 0.065 * PITCHES * np.random.randn(PITCHES, FRAMES)
    Gt = P * (D - (P * D).sum(axis=0, keepdims=True))
    g_words, g_scales = pack_weight(Gt * s[:, None], "e5m2")
    combs = harmonic_combs() + 0.1 * np.random.randn(BINS, PITCHES)
    bands = np.exp(0.8 * np.random.randn(BINS)[None, :] + 0.4 * np.random.randn(FRAMES, BINS))
    floor = 0.1 * np.exp(0.3 * np.random.randn(BINS))
    r = 0.5 * np.random.randn(FRAMES, BINS)
    return {"g_words": g_words, "g_scales": g_scales, "combs": bf(combs / s[None, :]),
            "bands": bf(bands), "floor": bf(floor), "r": bf(r)}

def reference(g_words, g_scales, combs, bands, floor, r):
    Gt = unpack_weight(g_words, g_scales, "e5m2")
    Cq = mxq(f64(combs), 1, "e4m3")
    dX = (Gt.T @ Cq.T) + f64(r)
    y = dX / (f64(bands) + f64(floor))
    Y = y.T
    words, scales = planes(Y)
    return y, words, scales

@@ -1,0 +1,382 @@
+from contextlib import ExitStack
+
+import concourse.mybir as mybir
+from concourse.masks import make_identity
+
+FRAMES, PITCHES, BINS = 1024, 1024, 2048
+FLOPS = 2 * FRAMES * PITCHES * BINS
+
+F32 = mybir.dt.float32
+BF16 = mybir.dt.bfloat16
+U32 = mybir.dt.uint32
+I32 = mybir.dt.int32
+U8 = mybir.dt.uint8
+E4M3 = mybir.dt.float8_e4m3fn_x4
+E5M2 = mybir.dt.float8_e5m2_x4
+ACT = mybir.ActivationFunctionType
+ALU = mybir.AluOpType
+
+P = 128
+W = 512
+PASSES = PITCHES // W
+GROUPS = BINS // W
+HALVES = FRAMES // W
+TILES = GROUPS * HALVES
+UNITS = TILES * 4
+PAIRS = UNITS // 2
+V_SQUARES = 0
+S_ROUND_FROM = 22
+G_ROUND = False
+V_YCOPY = 0
+V_CCOPY = 4
+C_LEAD = 5
+WARM = 0
+V_ROUND_FROM = 31
+
+
+def tile_salience_comb_backward_k2_kernel(
+    tc, g_words, g_scales, combs, bands, floor, r, out_0, out_1, out_2
+):
+    nc = tc.nc
+    with ExitStack() as ctx:
+        keep = ctx.enter_context(tc.tile_pool(name="keep", bufs=1))
+        work = ctx.enter_context(tc.tile_pool(name="work", bufs=2))
+        planes = ctx.enter_context(tc.tile_pool(name="planes", bufs=1))
+        psum = ctx.enter_context(tc.psum_pool(name="psum", bufs=1))
+        ctx.enter_context(tc.manual_schedule())
+
+        bank_bufs = {"mx": 3, "rec": 2, "bands": 1, "y": 1, "combs": 1}
+
+        def bank(tag):
+            return psum.tile([P, W], F32, name="bank_" + tag, tag=tag, bufs=bank_bufs[tag])
+
+        ident = keep.tile([P, P], F32, name="ident")
+        floor_rows = keep.tile([P, 2 * P], BF16, name="floor_rows")
+        floor_cols = keep.tile([P, 16], F32, name="floor_cols")
+        g_plane = keep.tile([P, PASSES, FRAMES], U8, name="g_plane", align_bytes=64)
+        y_plane = planes.tile([P, FRAMES], U8, name="y_plane", align_bytes=64)
+        warm = keep.tile([P, 8], F32, name="warm")
+
+        g_codes, bands_sb, r_sb, combs_sb = {}, {}, {}, {}
+        c_grouped, c_codes, c_scales = {}, {}, {}
+        c_bank, b_bank, y_bank, mx_bank, rec_bank = {}, {}, {}, {}, {}
+        rs, rec, num, y, y_bf, y_grouped, y_codes = {}, {}, {}, {}, {}, {}, {}
+
+        def place(m):
+            bg, fh = divmod(m, HALVES)
+            return slice(fh * W, (fh + 1) * W), slice(bg * W, (bg + 1) * W)
+
+        def load_g(fh):
+            g_codes[fh] = keep.tile([P, PASSES, W], U32, name="g_codes%d" % fh, align_bytes=64)
+            src = g_words[:, :, fh * W : (fh + 1) * W, :].rearrange("g p n t -> p g (n t)")
+            nc.sync.dma_start(out=g_codes[fh][:].bitcast(I32), in_=src.bitcast(I32))
+
+        def load_bands(m):
+            frames, bins = place(m)
+            bands_sb[m] = keep.tile([P, 4, W], BF16, name="bands%d" % m)
+            nc.sync.dma_start(out=bands_sb[m][:], in_=bands[frames, bins].rearrange("(i p) b -> p i b", p=P))
+
+        def load_r(m):
+            frames, bins = place(m)
+            r_sb[m] = keep.tile([P, 4, W], BF16, name="r%d" % m)
+            nc.sync.dma_start(out=r_sb[m][:], in_=r[frames, bins].rearrange("(i p) b -> p i b", p=P))
+
+        def load_combs(c):
+            bg, g = divmod(c, PASSES)
+            combs_sb[c] = keep.tile([P, 4, W], BF16, name="combs%d" % c)
+            block = combs[bg * W : (bg + 1) * W, g * W : (g + 1) * W]
+            nc.sync.dma_start(out=combs_sb[c][:], in_=block.rearrange("(j p) k -> p j k", p=P))
+
+        def turn_combs(c, h, tag):
+            c_bank[c, h] = bank(tag)
+            words = combs_sb[c][:].bitcast(F32)
+            for j in range(2):
+                for u in range(2):
+                    col = (2 * j + u) * P
+                    nc.tensor.transpose(c_bank[c, h][:, col : col + P], words[:, 2 * h + j, u:256:2], ident[:])
+
+        def copy_combs(c, h, on_vector):
+            if h == 0:
+                c_grouped[c] = work.tile([P, 4 * W], BF16, name="c_grouped", bufs=3, align_bytes=64)
+            dst = c_grouped[c][:].bitcast(F32)[:, h * W : (h + 1) * W].rearrange("k (j p u) -> k j p u", j=2, u=2)
+            src = c_bank[c, h][:].rearrange("k (j u p) -> k j p u", j=2, u=2)
+            if on_vector:
+                nc.vector.tensor_copy(out=dst, in_=src)
+            else:
+                nc.scalar.copy(out=dst, in_=src)
+
+        def quantize_combs(c):
+            bg, g = divmod(c, PASSES)
+            c_codes[bg, g] = work.tile([P, W], U32, name="c_codes", bufs=4, align_bytes=64)
+            c_scales[bg, g] = work.tile([P, W], U8, name="c_scales", bufs=4, align_bytes=64)
+            nc.vector.quantize_mx(
+                out=c_codes[bg, g][:].bitcast(E4M3), scales=c_scales[bg, g][:], in_=c_grouped[c][:]
+            )
+
+        def turn_bands(b, tag):
+            m, j = divmod(b, 2)
+            b_bank[b] = bank(tag)
+            words = bands_sb[m][:].bitcast(F32)
+            for i in range(4):
+                nc.tensor.transpose(b_bank[b][:, i * P : (i + 1) * P], words[:, i, j * P : (j + 1) * P], ident[:])
+
+        def inverse_root(b):
+            m, j = divmod(b, 2)
+            rs[b] = work.tile([P, 2, W], F32, name="rs", bufs=2)
+            src = b_bank[b][:].bitcast(BF16).rearrange("p (f e) -> p e f", e=2)
+            for e in range(2):
+                col = 2 * (2 * (m // HALVES) + j) + e
+                nc.scalar.activation(
+                    out=rs[b][:, e, :], in_=src[:, e, :], func=ACT.Abs_reciprocal_sqrt, bias=floor_cols[:, col : col + 1]
+                )
+
+        def square(b):
+            rec[b] = work.tile([P, 2, W], F32, name="rec", bufs=6)
+            if b < V_SQUARES:
+                nc.vector.tensor_tensor(out=rec[b][:], in0=rs[b][:], in1=rs[b][:], op=ALU.mult)
+            else:
+                nc.scalar.activation(out=rec[b][:], in_=rs[b][:], func=ACT.Square)
+
+        def turn_rec(n):
+            m, i = divmod(n, 4)
+            rec_bank[n] = bank("rec")
+            for j in range(2):
+                for e in range(2):
+                    col = (2 * j + e) * P
+                    nc.tensor.transpose(
+                        rec_bank[n][:, col : col + P], rec[2 * m + j][:, e, i * P : (i + 1) * P], ident[:]
+                    )
+
+        def product(n, g):
+            m, i = divmod(n, 4)
+            bg, fh = divmod(m, HALVES)
+            if g == 0:
+                mx_bank[n] = bank("mx")
+            f0 = fh * W + i * P
+            nc.tensor.matmul_mx(
+                out=mx_bank[n][:],
+                lhsT=g_codes[fh][:, g, i * P : (i + 1) * P].bitcast(E5M2),
+                lhsT_scale=g_plane[:, g, f0 : f0 + P],
+                rhs=c_codes[bg, g][:].bitcast(E4M3),
+                rhs_scale=c_scales[bg, g][:],
+                start=(g == 0),
+                stop=(g == PASSES - 1),
+            )
+
+        def add_r(n):
+            m, i = divmod(n, 4)
+            num[n] = work.tile([P, W], F32, name="num", bufs=3)
+            nc.vector.tensor_tensor(out=num[n][:], in0=mx_bank[n][:], in1=r_sb[m][:, i, :], op=ALU.add)
+
+        def divide(n):
+            q, i = divmod(n, 2)
+            if i == 0:
+                y[q] = work.tile([P, 2, W], F32, name="y", bufs=4)
+            nc.vector.tensor_tensor(
+                out=y[q][:, i, :].rearrange("f (j p e) -> f j p e", j=2, e=2),
+                in0=rec_bank[n][:].rearrange("f (j e p) -> f j p e", j=2, e=2),
+                in1=num[n][:].rearrange("f (j p e) -> f j p e", j=2, e=2),
+                op=ALU.mult,
+            )
+
+        def round_y(n):
+            q, i = divmod(n, 2)
+            y_bf[n] = work.tile([P, W], BF16, name="y_bf", bufs=4)
+            dst = y_bf[n][:].rearrange("f (u p e) -> f u p e", u=2, e=2)
+            src = y[q][:, i, :].rearrange("f (p u e) -> f u p e", u=2, e=2)
+            if S_ROUND_FROM <= n < V_ROUND_FROM:
+                nc.scalar.copy(out=dst, in_=src)
+            elif G_ROUND and n < V_ROUND_FROM:
+                nc.gpsimd.tensor_scalar(out=dst, in0=src, scalar1=1.0, scalar2=0.0, op0=ALU.mult, op1=ALU.add)
+            else:
+                nc.vector.tensor_copy(out=dst, in_=src)
+
+        def store_y(n0, count):
+            frames, bins = place(n0 // 4)
+            f0 = frames.start + (n0 % 4) * P
+            dst = out_0[f0 : f0 + count * P, bins].rearrange("(i p) b -> p i b", p=P)
+            nc.sync.dma_start(out=dst, in_=y[n0 // 2][:, n0 % 2 : n0 % 2 + count, :])
+
+        def turn_y(n0, count, tag):
+            y_bank[n0] = bank(tag)
+            for i in range(count):
+                words = y_bf[n0 + i][:].bitcast(F32)
+                for u in range(2):
+                    col = (2 * i + u) * P
+                    nc.tensor.transpose(y_bank[n0][:, col : col + P], words[:, u * P : (u + 1) * P], ident[:])
+
+        def y_on_vector(q):
+            return V_YCOPY > 0 and q % V_YCOPY == 0 and q < PAIRS - 4
+
+        def copy_y(n0, count):
+            y_grouped[n0] = work.tile([P, count * W], BF16, name="y_grouped", bufs=3, align_bytes=64)
+            dst = y_grouped[n0][:].bitcast(F32).rearrange("p (i m u) -> p i m u", i=count, u=2)
+            src = y_bank[n0][:, 0 : count * 2 * P].rearrange("p (i u m) -> p i m u", i=count, u=2)
+            if y_on_vector(n0 // 2):
+                nc.vector.tensor_copy(out=dst, in_=src)
+            else:
+                nc.scalar.copy(out=dst, in_=src)
+
+        def quantize_y(n0, count):
+            m, i = divmod(n0, 4)
+            bg, fh = divmod(m, HALVES)
+            if i == 0:
+                y_codes[m] = planes.tile([P, W], U32, name="y_codes", bufs=3, align_bytes=64)
+            f0 = fh * W + i * P
+            nc.vector.quantize_mx(
+                out=y_codes[m][:, i * P : (i + count) * P].bitcast(E4M3),
+                scales=y_plane[4 * bg : P, f0 : f0 + count * P],
+                in_=y_grouped[n0][:],
+            )
+
+        def store_codes(n0, count):
+            m, i = divmod(n0, 4)
+            bg, fh = divmod(m, HALVES)
+            f0 = fh * W + i * P
+            dst = out_1[bg, :, f0 : f0 + count * P, :].rearrange("p m t -> p (m t)")
+            nc.sync.dma_start(out=dst.bitcast(I32), in_=y_codes[m][:, i * P : (i + count) * P].bitcast(I32))
+
+        def store_scales(fh, queues):
+            cols = slice(fh * W, (fh + 1) * W)
+            for quad in range(4):
+                dst = out_2[:, 4 * quad : 4 * quad + 4, cols]
+                queues[quad % 2].dma_start(out=dst.bitcast(I32), in_=y_plane[32 * quad : 32 * quad + 16, cols].bitcast(I32))
+
+        nc.vector.memset(floor_rows[:], 0.0)
+        nc.vector.memset(g_plane[:].rearrange("p g n -> p (g n)").bitcast(I32), 0)
+        nc.vector.memset(warm[:], 1.0)
+        make_identity(nc, ident[:])
+        load_bands(0)
+        nc.sync.dma_start(out=floor_rows[0:8, :], in_=floor.rearrange("(j w) -> j w", j=8))
+        load_combs(0)
+        load_combs(1)
+        for quad in range(4):
+            src = g_scales[:, 4 * quad : 4 * quad + 4, :].rearrange("g r n -> r g n")
+            nc.scalar.dma_start(out=g_plane[32 * quad : 32 * quad + 4, :, :].bitcast(I32), in_=src.bitcast(I32))
+        nc.scalar.activation(out=warm[:, 4:8], in_=warm[:, 0:4], func=ACT.Abs_reciprocal_sqrt)
+        load_g(0)
+        load_bands(1)
+        load_r(0)
+        load_combs(2)
+        load_g(1)
+        load_r(1)
+        load_combs(3)
+        load_bands(2)
+
+        if WARM:
+            zeros = keep.tile([P, 4 * W], BF16, name="zeros", align_bytes=64)
+            w_codes = keep.tile([P, W + P], U32, name="w_codes", align_bytes=64)
+            w_scales = keep.tile([P, W + P], U8, name="w_scales", align_bytes=64)
+            nc.vector.memset(zeros[:].bitcast(I32), 0)
+            nc.vector.quantize_mx(out=w_codes[:, 0:W].bitcast(E4M3), scales=w_scales[:, 0:W], in_=zeros[:])
+            nc.vector.quantize_mx(out=w_codes[:, W:].bitcast(E5M2), scales=w_scales[:, W:], in_=zeros[:, 0:W])
+            warm_bank = bank("bands")
+            for k in range(WARM):
+                nc.tensor.matmul_mx(
+                    out=warm_bank[:], lhsT=w_codes[:, W:].bitcast(E5M2), lhsT_scale=w_scales[:, W:],
+                    rhs=w_codes[:, 0:W].bitcast(E4M3), rhs_scale=w_scales[:, 0:W], start=True, stop=True,
+                )
+
+        floor_bank = bank("y")
+        nc.tensor.transpose(floor_bank[:, 0:P], floor_rows[:].bitcast(F32), ident[:])
+        nc.vector.tensor_copy(out=floor_cols[:], in_=floor_bank[:].bitcast(BF16)[:, 0:16])
+        turn_bands(0, "rec")
+        turn_bands(1, "rec")
+        inverse_root(0)
+        inverse_root(1)
+        square(0)
+        head_banks = ("combs", "y", "mx", "combs")
+        for c in range(PASSES):
+            for h in range(2):
+                turn_combs(c, h, head_banks[2 * c + h])
+                copy_combs(c, h, True)
+            if c == 0:
+                square(1)
+            quantize_combs(c)
+        turn_bands(2, "bands")
+
+        def unit(n):
+            return 0 <= n < UNITS
+
+        def pair(q):
+            return 0 <= q < PAIRS
+
+        combs_jobs = {}
+        for bg in range(1, GROUPS):
+            for k in range(4):
+                combs_jobs.setdefault(max(4 * bg - C_LEAD + k, k - 1), []).append((2 * bg + k // 2, k % 2))
+
+        for q in range(-1, PAIRS):
+            a, b = 2 * q, 2 * q + 1
+            jobs = combs_jobs.get(q, [])
+            turned = combs_jobs.get(q - 1, [])
+            if q % 2 == 0 and (q + 4) // 2 < TILES:
+                load_r((q + 4) // 2)
+            if q % 2 == 1 and 4 + (q + 1) // 2 < 2 * GROUPS:
+                load_combs(4 + (q + 1) // 2)
+            if q % 2 == 1 and (q + 7) // 2 < TILES:
+                load_bands((q + 7) // 2)
+            if unit(a + 2):
+                for g in range(PASSES):
+                    product(a + 2, g)
+                    product(a + 3, g)
+            for c, h in jobs[:1]:
+                turn_combs(c, h, "combs")
+            if unit(b):
+                turn_rec(b)
+            if pair(q + 3):
+                inverse_root(q + 3)
+            if pair(q + 4):
+                turn_bands(q + 4, "bands")
+            if unit(b):
+                add_r(b)
+            if unit(a):
+                divide(a)
+                if q == PAIRS - 1:
+                    store_y(a, 1)
+            if unit(a - 1):
+                round_y(a - 1)
+            if pair(q - 2):
+                copy_y(a - 4, 2)
+            if pair(q + 3):
+                square(q + 3)
+            for c, h in jobs[:1]:
+                copy_combs(c, h, 2 * c + h < V_CCOPY)
+            if unit(b + 1):
+                turn_rec(b + 1)
+                add_r(b + 1)
+            if unit(b):
+                divide(b)
+                if q < PAIRS - 1:
+                    store_y(a, 2)
+            for c, h in (jobs if q == 2 or C_LEAD == 5 else turned if q != 3 else []):
+                if h == 1:
+                    quantize_combs(c)
+            if pair(q - 2):
+                quantize_y(a - 4, 2)
+                if q % 2 == 1:
+                    store_codes(a - 6, 4)
+                if q == PAIRS - 1:
+                    store_scales(0, (nc.sync, nc.sync))
+            if unit(a):
+                round_y(a)
+            if pair(q - 1):
+                turn_y(a - 2, 2, "y")
+            for c, h in jobs[1:]:
+                turn_combs(c, h, "combs")
+                copy_combs(c, h, 2 * c + h < V_CCOPY)
+
+        last = UNITS - 1
+        store_y(last, 1)
+        round_y(last)
+        copy_y(last - 3, 2)
+        turn_y(last - 1, 1, "bands")
+        turn_y(last, 1, "combs")
+        copy_y(last - 1, 1)
+        quantize_y(last - 3, 2)
+        store_codes(last - 3, 2)
+        copy_y(last, 1)
+        quantize_y(last - 1, 1)
+        quantize_y(last, 1)
+        store_codes(last - 1, 2)
+        store_scales(1, (nc.scalar, nc.sync))

@@ -25,12 +25,19 @@ TILES = GROUPS * HALVES
 UNITS = TILES * 4
 PAIRS = UNITS // 2
 V_SQUARES = 0
-S_ROUND_FROM = 22
-G_ROUND = False
-V_YCOPY = 0
+S_ROUND_FROM = 32
+G_ROUND = True
+V_YCOPY = 2
 V_CCOPY = 4
 C_LEAD = 5
 WARM = 0
+LOADS = 2
+B_LEAD = 2
+Y_UNTIL = 9
+BURST = False
+MXB = 3
+YB = 1
+RB = 2
 V_ROUND_FROM = 31
 
 
@@ -45,7 +52,7 @@ def tile_salience_comb_backward_k2_kernel(
         psum = ctx.enter_context(tc.psum_pool(name="psum", bufs=1))
         ctx.enter_context(tc.manual_schedule())
 
-        bank_bufs = {"mx": 3, "rec": 2, "bands": 1, "y": 1, "combs": 1}
+        bank_bufs = {"mx": MXB, "rec": RB, "bands": 1, "y": YB, "combs": 1}
 
         def bank(tag):
             return psum.tile([P, W], F32, name="bank_" + tag, tag=tag, bufs=bank_bufs[tag])
@@ -206,7 +213,7 @@ def tile_salience_comb_backward_k2_kernel(
                     nc.tensor.transpose(y_bank[n0][:, col : col + P], words[:, u * P : (u + 1) * P], ident[:])
 
         def y_on_vector(q):
-            return V_YCOPY > 0 and q % V_YCOPY == 0 and q < PAIRS - 4
+            return V_YCOPY > 0 and q % V_YCOPY == 0 and q < Y_UNTIL
 
         def copy_y(n0, count):
             y_grouped[n0] = work.tile([P, count * W], BF16, name="y_grouped", bufs=3, align_bytes=64)
@@ -252,15 +259,15 @@ def tile_salience_comb_backward_k2_kernel(
         load_combs(1)
         for quad in range(4):
             src = g_scales[:, 4 * quad : 4 * quad + 4, :].rearrange("g r n -> r g n")
-            nc.scalar.dma_start(out=g_plane[32 * quad : 32 * quad + 4, :, :].bitcast(I32), in_=src.bitcast(I32))
+            nc.gpsimd.dma_start(out=g_plane[32 * quad : 32 * quad + 4, :, :].bitcast(I32), in_=src.bitcast(I32))
         nc.scalar.activation(out=warm[:, 4:8], in_=warm[:, 0:4], func=ACT.Abs_reciprocal_sqrt)
         load_g(0)
-        load_bands(1)
         load_r(0)
+        load_bands(1)
         load_combs(2)
         load_g(1)
-        load_r(1)
         load_combs(3)
+        load_r(1)
         load_bands(2)
 
         if WARM:
@@ -293,7 +300,8 @@ def tile_salience_comb_backward_k2_kernel(
             if c == 0:
                 square(1)
             quantize_combs(c)
-        turn_bands(2, "bands")
+        if B_LEAD == 3:
+            turn_bands(2, "bands")
 
         def unit(n):
             return 0 <= n < UNITS
@@ -306,28 +314,31 @@ def tile_salience_comb_backward_k2_kernel(
             for k in range(4):
                 combs_jobs.setdefault(max(4 * bg - C_LEAD + k, k - 1), []).append((2 * bg + k // 2, k % 2))
 
+        loads = []
+        for m in range(2, TILES):
+            loads.append((load_r, m))
+            if m + 2 < TILES:
+                loads.append((load_combs, m + 2))
+            if m + 1 < TILES:
+                loads.append((load_bands, m + 1))
+
         for q in range(-1, PAIRS):
             a, b = 2 * q, 2 * q + 1
             jobs = combs_jobs.get(q, [])
             turned = combs_jobs.get(q - 1, [])
-            if q % 2 == 0 and (q + 4) // 2 < TILES:
-                load_r((q + 4) // 2)
-            if q % 2 == 1 and 4 + (q + 1) // 2 < 2 * GROUPS:
-                load_combs(4 + (q + 1) // 2)
-            if q % 2 == 1 and (q + 7) // 2 < TILES:
-                load_bands((q + 7) // 2)
+            for job in loads[LOADS * (q + 1) : LOADS * (q + 2)]:
+                job[0](job[1])
             if unit(a + 2):
                 for g in range(PASSES):
                     product(a + 2, g)
-                    product(a + 3, g)
+                    if BURST:
+                        product(a + 3, g)
             for c, h in jobs[:1]:
                 turn_combs(c, h, "combs")
             if unit(b):
                 turn_rec(b)
-            if pair(q + 3):
-                inverse_root(q + 3)
-            if pair(q + 4):
-                turn_bands(q + 4, "bands")
+            if 2 <= q + B_LEAD < PAIRS:
+                inverse_root(q + B_LEAD)
             if unit(b):
                 add_r(b)
             if unit(a):
@@ -338,10 +349,15 @@ def tile_salience_comb_backward_k2_kernel(
                 round_y(a - 1)
             if pair(q - 2):
                 copy_y(a - 4, 2)
-            if pair(q + 3):
-                square(q + 3)
+            if 2 <= q + B_LEAD < PAIRS:
+                square(q + B_LEAD)
             for c, h in jobs[:1]:
                 copy_combs(c, h, 2 * c + h < V_CCOPY)
+            if unit(b + 2) and not BURST:
+                for g in range(PASSES):
+                    product(b + 2, g)
+            if B_LEAD <= q + B_LEAD + 1 < PAIRS:
+                turn_bands(q + B_LEAD + 1, "bands")
             if unit(b + 1):
                 turn_rec(b + 1)
                 add_r(b + 1)

@@ -31,7 +31,9 @@ V_YCOPY = 2
 V_CCOPY = 4
 C_LEAD = 5
 WARM = 0
-LOADS = 2
+LOADS = 20
+WIDE = 1
+Y_BUFS = 9
 B_LEAD = 2
 Y_UNTIL = 9
 BURST = False
@@ -78,35 +80,41 @@ def tile_salience_comb_backward_k2_kernel(
             src = g_words[:, :, fh * W : (fh + 1) * W, :].rearrange("g p n t -> p g (n t)")
             nc.sync.dma_start(out=g_codes[fh][:].bitcast(I32), in_=src.bitcast(I32))
 
-        def load_bands(m):
-            frames, bins = place(m)
-            bands_sb[m] = keep.tile([P, 4, W], BF16, name="bands%d" % m)
-            nc.sync.dma_start(out=bands_sb[m][:], in_=bands[frames, bins].rearrange("(i p) b -> p i b", p=P))
+        def load_block(src, store, label, fh, bg, count):
+            frames = slice(fh * W, (fh + 1) * W)
+            block = keep.tile([P, 4, count * W], BF16, name="%s%d%d" % (label, fh, bg))
+            cols = src[frames, bg * W : (bg + count) * W]
+            nc.sync.dma_start(out=block[:], in_=cols.rearrange("(i p) b -> p i b", p=P))
+            for k in range(count):
+                store[(bg + k) * HALVES + fh] = (block, k)
 
-        def load_r(m):
-            frames, bins = place(m)
-            r_sb[m] = keep.tile([P, 4, W], BF16, name="r%d" % m)
-            nc.sync.dma_start(out=r_sb[m][:], in_=r[frames, bins].rearrange("(i p) b -> p i b", p=P))
+        def load_bands(fh, bg, count):
+            load_block(bands, bands_sb, "bands", fh, bg, count)
+
+        def load_r(fh, bg, count):
+            load_block(r, r_sb, "r", fh, bg, count)
 
         def load_combs(c):
-            bg, g = divmod(c, PASSES)
-            combs_sb[c] = keep.tile([P, 4, W], BF16, name="combs%d" % c)
-            block = combs[bg * W : (bg + 1) * W, g * W : (g + 1) * W]
-            nc.sync.dma_start(out=combs_sb[c][:], in_=block.rearrange("(j p) k -> p j k", p=P))
+            combs_sb[c] = keep.tile([P, 2, PITCHES], BF16, name="combs%d" % c)
+            rows = combs[c * 256 : (c + 1) * 256, :]
+            nc.sync.dma_start(out=combs_sb[c][:], in_=rows.rearrange("(p j) k -> p j k", j=2))
 
-        def turn_combs(c, h, tag):
-            c_bank[c, h] = bank(tag)
+        def turn_combs(c, g, tag):
+            c_bank[c, g] = bank(tag)
             words = combs_sb[c][:].bitcast(F32)
             for j in range(2):
                 for u in range(2):
                     col = (2 * j + u) * P
-                    nc.tensor.transpose(c_bank[c, h][:, col : col + P], words[:, 2 * h + j, u:256:2], ident[:])
+                    nc.tensor.transpose(
+                        c_bank[c, g][:, col : col + P], words[:, j, 256 * g + u : 256 * (g + 1) : 2], ident[:]
+                    )
 
-        def copy_combs(c, h, on_vector):
+        def copy_combs(c, g, on_vector):
+            bg, h = divmod(c, 2)
             if h == 0:
-                c_grouped[c] = work.tile([P, 4 * W], BF16, name="c_grouped", bufs=3, align_bytes=64)
-            dst = c_grouped[c][:].bitcast(F32)[:, h * W : (h + 1) * W].rearrange("k (j p u) -> k j p u", j=2, u=2)
-            src = c_bank[c, h][:].rearrange("k (j u p) -> k j p u", j=2, u=2)
+                c_grouped[2 * bg + g] = work.tile([P, 4 * W], BF16, name="c_grouped", bufs=3, align_bytes=64)
+            dst = c_grouped[2 * bg + g][:].bitcast(F32)[:, h * W : (h + 1) * W].rearrange("k (p v) -> k p v", v=4)
+            src = c_bank[c, g][:].rearrange("k (v p) -> k p v", v=4)
             if on_vector:
                 nc.vector.tensor_copy(out=dst, in_=src)
             else:
@@ -123,7 +131,8 @@ def tile_salience_comb_backward_k2_kernel(
         def turn_bands(b, tag):
             m, j = divmod(b, 2)
             b_bank[b] = bank(tag)
-            words = bands_sb[m][:].bitcast(F32)
+            block, k = bands_sb[m]
+            words = block[:].bitcast(F32)[:, :, k * 256 : (k + 1) * 256]
             for i in range(4):
                 nc.tensor.transpose(b_bank[b][:, i * P : (i + 1) * P], words[:, i, j * P : (j + 1) * P], ident[:])
 
@@ -172,13 +181,14 @@ def tile_salience_comb_backward_k2_kernel(
 
         def add_r(n):
             m, i = divmod(n, 4)
+            block, k = r_sb[m]
             num[n] = work.tile([P, W], F32, name="num", bufs=3)
-            nc.vector.tensor_tensor(out=num[n][:], in0=mx_bank[n][:], in1=r_sb[m][:, i, :], op=ALU.add)
+            nc.vector.tensor_tensor(out=num[n][:], in0=mx_bank[n][:], in1=block[:, i, k * W : (k + 1) * W], op=ALU.add)
 
         def divide(n):
             q, i = divmod(n, 2)
             if i == 0:
-                y[q] = work.tile([P, 2, W], F32, name="y", bufs=4)
+                y[q] = work.tile([P, 2, W], F32, name="y", bufs=Y_BUFS)
             nc.vector.tensor_tensor(
                 out=y[q][:, i, :].rearrange("f (j p e) -> f j p e", j=2, e=2),
                 in0=rec_bank[n][:].rearrange("f (j e p) -> f j p e", j=2, e=2),
@@ -227,11 +237,11 @@ def tile_salience_comb_backward_k2_kernel(
         def quantize_y(n0, count):
             m, i = divmod(n0, 4)
             bg, fh = divmod(m, HALVES)
-            if i == 0:
-                y_codes[m] = planes.tile([P, W], U32, name="y_codes", bufs=3, align_bytes=64)
+            if i == 0 and fh == 0:
+                y_codes[bg] = planes.tile([P, FRAMES], U32, name="y_codes", bufs=2, align_bytes=64)
             f0 = fh * W + i * P
             nc.vector.quantize_mx(
-                out=y_codes[m][:, i * P : (i + count) * P].bitcast(E4M3),
+                out=y_codes[bg][:, f0 : f0 + count * P].bitcast(E4M3),
                 scales=y_plane[4 * bg : P, f0 : f0 + count * P],
                 in_=y_grouped[n0][:],
             )
@@ -241,7 +251,7 @@ def tile_salience_comb_backward_k2_kernel(
             bg, fh = divmod(m, HALVES)
             f0 = fh * W + i * P
             dst = out_1[bg, :, f0 : f0 + count * P, :].rearrange("p m t -> p (m t)")
-            nc.sync.dma_start(out=dst.bitcast(I32), in_=y_codes[m][:, i * P : (i + count) * P].bitcast(I32))
+            nc.sync.dma_start(out=dst.bitcast(I32), in_=y_codes[bg][:, f0 : f0 + count * P].bitcast(I32))
 
         def store_scales(fh, queues):
             cols = slice(fh * W, (fh + 1) * W)
@@ -253,22 +263,33 @@ def tile_salience_comb_backward_k2_kernel(
         nc.vector.memset(g_plane[:].rearrange("p g n -> p (g n)").bitcast(I32), 0)
         nc.vector.memset(warm[:], 1.0)
         make_identity(nc, ident[:])
-        load_bands(0)
+        load_bands(0, 0, 1)
         nc.sync.dma_start(out=floor_rows[0:8, :], in_=floor.rearrange("(j w) -> j w", j=8))
         load_combs(0)
         load_combs(1)
         for quad in range(4):
             src = g_scales[:, 4 * quad : 4 * quad + 4, :].rearrange("g r n -> r g n")
-            nc.gpsimd.dma_start(out=g_plane[32 * quad : 32 * quad + 4, :, :].bitcast(I32), in_=src.bitcast(I32))
+            nc.scalar.dma_start(out=g_plane[32 * quad : 32 * quad + 4, :, :].bitcast(I32), in_=src.bitcast(I32))
         nc.scalar.activation(out=warm[:, 4:8], in_=warm[:, 0:4], func=ACT.Abs_reciprocal_sqrt)
         load_g(0)
-        load_r(0)
-        load_bands(1)
-        load_combs(2)
-        load_g(1)
-        load_combs(3)
-        load_r(1)
-        load_bands(2)
+        load_r(0, 0, 1)
+        if WIDE == 2:
+            load_bands(1, 0, 2)
+            load_combs(2)
+            load_g(1)
+            load_r(1, 0, 2)
+            load_combs(3)
+            load_bands(0, 1, 1)
+            loads = [(load_r, 0, 1, 1), (load_combs, 4)]
+        else:
+            load_bands(1, 0, 1)
+            load_combs(2)
+            load_g(1)
+            load_r(1, 0, 1)
+            load_combs(3)
+            load_bands(0, 1, 1)
+            loads = [(load_combs, 4), (load_bands, 1, 1, 1), (load_r, 0, 1, 1), (load_r, 1, 1, 1)]
+        loads.extend([(load_combs, 5), (load_bands, 0, 2, 2), (load_combs, 6), (load_r, 0, 2, 2), (load_bands, 1, 2, 2), (load_combs, 7), (load_r, 1, 2, 2)])
 
         if WARM:
             zeros = keep.tile([P, 4 * W], BF16, name="zeros", align_bytes=64)
@@ -293,13 +314,14 @@ def tile_salience_comb_backward_k2_kernel(
         inverse_root(1)
         square(0)
         head_banks = ("combs", "y", "mx", "combs")
-        for c in range(PASSES):
-            for h in range(2):
-                turn_combs(c, h, head_banks[2 * c + h])
-                copy_combs(c, h, True)
+        for c in range(2):
+            for g in range(PASSES):
+                turn_combs(c, g, head_banks[2 * c + g])
+                copy_combs(c, g, True)
+                if c == 1:
+                    quantize_combs(g)
             if c == 0:
                 square(1)
-            quantize_combs(c)
         if B_LEAD == 3:
             turn_bands(2, "bands")
 
@@ -314,20 +336,12 @@ def tile_salience_comb_backward_k2_kernel(
             for k in range(4):
                 combs_jobs.setdefault(max(4 * bg - C_LEAD + k, k - 1), []).append((2 * bg + k // 2, k % 2))
 
-        loads = []
-        for m in range(2, TILES):
-            loads.append((load_r, m))
-            if m + 2 < TILES:
-                loads.append((load_combs, m + 2))
-            if m + 1 < TILES:
-                loads.append((load_bands, m + 1))
-
         for q in range(-1, PAIRS):
             a, b = 2 * q, 2 * q + 1
             jobs = combs_jobs.get(q, [])
             turned = combs_jobs.get(q - 1, [])
             for job in loads[LOADS * (q + 1) : LOADS * (q + 2)]:
-                job[0](job[1])
+                job[0](*job[1:])
             if unit(a + 2):
                 for g in range(PASSES):
                     product(a + 2, g)
@@ -365,12 +379,14 @@ def tile_salience_comb_backward_k2_kernel(
                 divide(b)
                 if q < PAIRS - 1:
                     store_y(a, 2)
-            for c, h in (jobs if q == 2 or C_LEAD == 5 else turned if q != 3 else []):
-                if h == 1:
-                    quantize_combs(c)
+            for c, g in jobs:
+                if c % 2 == 1:
+                    quantize_combs(c - 1 + g)
             if pair(q - 2):
                 quantize_y(a - 4, 2)
-                if q % 2 == 1:
+                if q % 4 == 1 and q > 1:
+                    store_codes(a - 10, 8)
+                if q == PAIRS - 1:
                     store_codes(a - 6, 4)
                 if q == PAIRS - 1:
                     store_scales(0, (nc.sync, nc.sync))

@@ -29,18 +29,27 @@ S_ROUND_FROM = 32
 G_ROUND = True
 V_YCOPY = 2
 V_CCOPY = 4
-C_LEAD = 5
+C_LEAD = 6
 WARM = 0
-LOADS = 20
-WIDE = 1
+LOADS = 2
+W0 = 2
+W3 = 1
+HV1 = True
+HV3 = False
+TAILV = False
+W1 = 1
+W2 = 3
+EARLY = True
+Q_STEP = 0
+B_FIRST = False
 Y_BUFS = 9
-B_LEAD = 2
-Y_UNTIL = 9
-BURST = False
+B_LEAD = 3
+Y_UNTIL = 7
+BURST = True
 MXB = 3
 YB = 1
 RB = 2
-V_ROUND_FROM = 31
+V_ROUND_FROM = 30
 
 
 def tile_salience_comb_backward_k2_kernel(
@@ -225,11 +234,11 @@ def tile_salience_comb_backward_k2_kernel(
         def y_on_vector(q):
             return V_YCOPY > 0 and q % V_YCOPY == 0 and q < Y_UNTIL
 
-        def copy_y(n0, count):
-            y_grouped[n0] = work.tile([P, count * W], BF16, name="y_grouped", bufs=3, align_bytes=64)
+        def copy_y(n0, count, on_vector):
+            y_grouped[n0] = work.tile([P, count * W], BF16, name="y_grouped", bufs=4, align_bytes=64)
             dst = y_grouped[n0][:].bitcast(F32).rearrange("p (i m u) -> p i m u", i=count, u=2)
             src = y_bank[n0][:, 0 : count * 2 * P].rearrange("p (i u m) -> p i m u", i=count, u=2)
-            if y_on_vector(n0 // 2):
+            if on_vector:
                 nc.vector.tensor_copy(out=dst, in_=src)
             else:
                 nc.scalar.copy(out=dst, in_=src)
@@ -253,16 +262,34 @@ def tile_salience_comb_backward_k2_kernel(
             dst = out_1[bg, :, f0 : f0 + count * P, :].rearrange("p m t -> p (m t)")
             nc.sync.dma_start(out=dst.bitcast(I32), in_=y_codes[bg][:, f0 : f0 + count * P].bitcast(I32))
 
-        def store_scales(fh, queues):
-            cols = slice(fh * W, (fh + 1) * W)
+        def store_scales(queues):
+            cols = slice(0, FRAMES)
             for quad in range(4):
                 dst = out_2[:, 4 * quad : 4 * quad + 4, cols]
                 queues[quad % 2].dma_start(out=dst.bitcast(I32), in_=y_plane[32 * quad : 32 * quad + 16, cols].bitcast(I32))
 
         nc.vector.memset(floor_rows[:], 0.0)
-        nc.vector.memset(g_plane[:].rearrange("p g n -> p (g n)").bitcast(I32), 0)
-        nc.vector.memset(warm[:], 1.0)
         make_identity(nc, ident[:])
+        nc.vector.memset(warm[:], 1.0)
+        nc.scalar.activation(out=warm[:, 4:8], in_=warm[:, 0:4], func=ACT.Abs_reciprocal_sqrt)
+        if WARM:
+            zeros = keep.tile([P, 4 * W], BF16, name="zeros", align_bytes=64)
+            w_codes = keep.tile([P, W + P], U32, name="w_codes", align_bytes=64)
+            w_scales = keep.tile([P, W + P], U8, name="w_scales", align_bytes=64)
+            nc.vector.memset(zeros[:].bitcast(I32), 0)
+        nc.vector.memset(g_plane[:].rearrange("p g n -> p (g n)").bitcast(I32), 0)
+        if WARM:
+            nc.vector.quantize_mx(out=w_codes[:, W:].bitcast(E5M2), scales=w_scales[:, W:], in_=zeros[:, 0:W])
+            nc.vector.quantize_mx(out=w_codes[:, 0:W].bitcast(E4M3), scales=w_scales[:, 0:W], in_=zeros[:])
+            warm_bank = bank("mx")
+
+        def warm_up(count):
+            for k in range(count if WARM else 0):
+                nc.tensor.matmul_mx(
+                    out=warm_bank[:], lhsT=w_codes[:, W:].bitcast(E5M2), lhsT_scale=w_scales[:, W:],
+                    rhs=w_codes[:, 0:W].bitcast(E4M3), rhs_scale=w_scales[:, 0:W], start=True, stop=True,
+                )
+
         load_bands(0, 0, 1)
         nc.sync.dma_start(out=floor_rows[0:8, :], in_=floor.rearrange("(j w) -> j w", j=8))
         load_combs(0)
@@ -270,60 +297,52 @@ def tile_salience_comb_backward_k2_kernel(
         for quad in range(4):
             src = g_scales[:, 4 * quad : 4 * quad + 4, :].rearrange("g r n -> r g n")
             nc.scalar.dma_start(out=g_plane[32 * quad : 32 * quad + 4, :, :].bitcast(I32), in_=src.bitcast(I32))
-        nc.scalar.activation(out=warm[:, 4:8], in_=warm[:, 0:4], func=ACT.Abs_reciprocal_sqrt)
+        load_bands(1, 0, 1)
         load_g(0)
+        load_combs(2)
         load_r(0, 0, 1)
-        if WIDE == 2:
-            load_bands(1, 0, 2)
-            load_combs(2)
-            load_g(1)
-            load_r(1, 0, 2)
-            load_combs(3)
-            load_bands(0, 1, 1)
-            loads = [(load_r, 0, 1, 1), (load_combs, 4)]
-        else:
-            load_bands(1, 0, 1)
-            load_combs(2)
-            load_g(1)
-            load_r(1, 0, 1)
-            load_combs(3)
-            load_bands(0, 1, 1)
-            loads = [(load_combs, 4), (load_bands, 1, 1, 1), (load_r, 0, 1, 1), (load_r, 1, 1, 1)]
-        loads.extend([(load_combs, 5), (load_bands, 0, 2, 2), (load_combs, 6), (load_r, 0, 2, 2), (load_bands, 1, 2, 2), (load_combs, 7), (load_r, 1, 2, 2)])
+        load_combs(3)
+        load_bands(0, 1, 1)
+        load_g(1)
+        load_r(1, 0, 1)
+        load_combs(4)
+        load_bands(1, 1, 1)
+        load_r(0, 1, 1)
+        load_combs(5)
+        load_bands(0, 2, 2)
+        load_r(1, 1, 1)
+        load_combs(6)
+        load_bands(1, 2, 2)
+        load_r(0, 2, 2)
+        load_combs(7)
+        load_r(1, 2, 2)
 
-        if WARM:
-            zeros = keep.tile([P, 4 * W], BF16, name="zeros", align_bytes=64)
-            w_codes = keep.tile([P, W + P], U32, name="w_codes", align_bytes=64)
-            w_scales = keep.tile([P, W + P], U8, name="w_scales", align_bytes=64)
-            nc.vector.memset(zeros[:].bitcast(I32), 0)
-            nc.vector.quantize_mx(out=w_codes[:, 0:W].bitcast(E4M3), scales=w_scales[:, 0:W], in_=zeros[:])
-            nc.vector.quantize_mx(out=w_codes[:, W:].bitcast(E5M2), scales=w_scales[:, W:], in_=zeros[:, 0:W])
-            warm_bank = bank("bands")
-            for k in range(WARM):
-                nc.tensor.matmul_mx(
-                    out=warm_bank[:], lhsT=w_codes[:, W:].bitcast(E5M2), lhsT_scale=w_scales[:, W:],
-                    rhs=w_codes[:, 0:W].bitcast(E4M3), rhs_scale=w_scales[:, 0:W], start=True, stop=True,
-                )
-
+        warm_up(W0)
         floor_bank = bank("y")
         nc.tensor.transpose(floor_bank[:, 0:P], floor_rows[:].bitcast(F32), ident[:])
         nc.vector.tensor_copy(out=floor_cols[:], in_=floor_bank[:].bitcast(BF16)[:, 0:16])
         turn_bands(0, "rec")
-        turn_bands(1, "rec")
+        warm_up(W1)
         inverse_root(0)
-        inverse_root(1)
+        turn_combs(0, 0, "combs")
+        copy_combs(0, 0, True)
+        turn_combs(0, 1, "y")
         square(0)
-        head_banks = ("combs", "y", "mx", "combs")
-        for c in range(2):
-            for g in range(PASSES):
-                turn_combs(c, g, head_banks[2 * c + g])
-                copy_combs(c, g, True)
-                if c == 1:
-                    quantize_combs(g)
-            if c == 0:
-                square(1)
-        if B_LEAD == 3:
-            turn_bands(2, "bands")
+        copy_combs(0, 1, HV1)
+        warm_up(W3)
+        turn_combs(1, 0, "mx")
+        copy_combs(1, 0, True)
+        turn_combs(1, 1, "combs")
+        copy_combs(1, 1, HV3)
+        quantize_combs(0)
+        quantize_combs(1)
+        turn_bands(1, "rec")
+        inverse_root(1)
+        turn_bands(2, "bands")
+        warm_up(W2)
+        if EARLY:
+            turn_combs(2, 0, "y")
+            copy_combs(2, 0, True)
 
         def unit(n):
             return 0 <= n < UNITS
@@ -334,62 +353,63 @@ def tile_salience_comb_backward_k2_kernel(
         combs_jobs = {}
         for bg in range(1, GROUPS):
             for k in range(4):
-                combs_jobs.setdefault(max(4 * bg - C_LEAD + k, k - 1), []).append((2 * bg + k // 2, k % 2))
+                if (bg, k) != (1, 0) or not EARLY:
+                    combs_jobs.setdefault(max(4 * bg - C_LEAD + k, -1), []).append((2 * bg + k // 2, k % 2))
 
         for q in range(-1, PAIRS):
             a, b = 2 * q, 2 * q + 1
             jobs = combs_jobs.get(q, [])
             turned = combs_jobs.get(q - 1, [])
-            for job in loads[LOADS * (q + 1) : LOADS * (q + 2)]:
-                job[0](*job[1:])
             if unit(a + 2):
-                for g in range(PASSES):
-                    product(a + 2, g)
-                    if BURST:
-                        product(a + 3, g)
+                for n in ((a + 2, a + 3) if BURST else (a + 2,)):
+                    for g in range(PASSES):
+                        product(n, g)
             for c, h in jobs[:1]:
                 turn_combs(c, h, "combs")
             if unit(b):
                 turn_rec(b)
-            if 2 <= q + B_LEAD < PAIRS:
-                inverse_root(q + B_LEAD)
+            if pair(q + 2):
+                square(q + 2)
+            if pair(q + 3):
+                inverse_root(q + 3)
             if unit(b):
                 add_r(b)
             if unit(a):
                 divide(a)
                 if q == PAIRS - 1:
                     store_y(a, 1)
+            if Q_STEP == 0:
+                for c, g in turned:
+                    if c % 2 == 1:
+                        quantize_combs(c - 1 + g)
             if unit(a - 1):
                 round_y(a - 1)
             if pair(q - 2):
-                copy_y(a - 4, 2)
-            if 2 <= q + B_LEAD < PAIRS:
-                square(q + B_LEAD)
+                copy_y(a - 4, 2, y_on_vector(q - 2))
             for c, h in jobs[:1]:
                 copy_combs(c, h, 2 * c + h < V_CCOPY)
             if unit(b + 2) and not BURST:
                 for g in range(PASSES):
                     product(b + 2, g)
-            if B_LEAD <= q + B_LEAD + 1 < PAIRS:
-                turn_bands(q + B_LEAD + 1, "bands")
+            if B_FIRST and pair(q + 4):
+                turn_bands(q + 4, "bands")
             if unit(b + 1):
                 turn_rec(b + 1)
                 add_r(b + 1)
+            if not B_FIRST and pair(q + 4):
+                turn_bands(q + 4, "bands")
             if unit(b):
                 divide(b)
                 if q < PAIRS - 1:
                     store_y(a, 2)
-            for c, g in jobs:
-                if c % 2 == 1:
-                    quantize_combs(c - 1 + g)
-            if pair(q - 2):
+            if Q_STEP == 1:
+                for c, g in turned:
+                    if c % 2 == 1:
+                        quantize_combs(c - 1 + g)
+            if pair(q - 2) and q < PAIRS - 1:
                 quantize_y(a - 4, 2)
                 if q % 4 == 1 and q > 1:
                     store_codes(a - 10, 8)
-                if q == PAIRS - 1:
-                    store_codes(a - 6, 4)
-                if q == PAIRS - 1:
-                    store_scales(0, (nc.sync, nc.sync))
             if unit(a):
                 round_y(a)
             if pair(q - 1):
@@ -401,14 +421,16 @@ def tile_salience_comb_backward_k2_kernel(
         last = UNITS - 1
         store_y(last, 1)
         round_y(last)
-        copy_y(last - 3, 2)
+        copy_y(last - 3, 2, False)
         turn_y(last - 1, 1, "bands")
         turn_y(last, 1, "combs")
-        copy_y(last - 1, 1)
+        quantize_y(last - 5, 2)
+        store_codes(last - 7, 4)
+        copy_y(last - 1, 1, False)
         quantize_y(last - 3, 2)
         store_codes(last - 3, 2)
-        copy_y(last, 1)
+        copy_y(last, 1, TAILV)
         quantize_y(last - 1, 1)
         quantize_y(last, 1)
         store_codes(last - 1, 2)
-        store_scales(1, (nc.scalar, nc.sync))
+        store_scales((nc.scalar, nc.sync))

from contextlib import ExitStack

import concourse.mybir as mybir
from concourse.masks import make_identity

FRAMES, PITCHES, BINS = 1024, 1024, 2048
FLOPS = 2 * FRAMES * PITCHES * BINS

F32 = mybir.dt.float32
BF16 = mybir.dt.bfloat16
U32 = mybir.dt.uint32
I32 = mybir.dt.int32
U8 = mybir.dt.uint8
E4M3 = mybir.dt.float8_e4m3fn_x4
E5M2 = mybir.dt.float8_e5m2_x4
ACT = mybir.ActivationFunctionType
ALU = mybir.AluOpType

P = 128
W = 512
PASSES = PITCHES // W
GROUPS = BINS // W
HALVES = FRAMES // W
TILES = GROUPS * HALVES
UNITS = TILES * 4
PAIRS = UNITS // 2
V_SQUARES = 0
S_ROUND_FROM = 32
G_ROUND = True
V_YCOPY = 2
V_CCOPY = 4
C_LEAD = 6
WARM = 0
LOADS = 2
W0 = 2
W3 = 1
HV1 = True
HV3 = False
TAILV = False
W1 = 1
W2 = 3
EARLY = True
Q_STEP = 0
B_FIRST = False
Y_BUFS = 9
B_LEAD = 3
Y_UNTIL = 7
BURST = True
MXB = 3
YB = 1
RB = 2
V_ROUND_FROM = 30


def tile_salience_comb_backward_k2_kernel(
    tc, g_words, g_scales, combs, bands, floor, r, out_0, out_1, out_2
):
    nc = tc.nc
    with ExitStack() as ctx:
        keep = ctx.enter_context(tc.tile_pool(name="keep", bufs=1))
        work = ctx.enter_context(tc.tile_pool(name="work", bufs=2))
        planes = ctx.enter_context(tc.tile_pool(name="planes", bufs=1))
        psum = ctx.enter_context(tc.psum_pool(name="psum", bufs=1))
        ctx.enter_context(tc.manual_schedule())

        bank_bufs = {"mx": MXB, "rec": RB, "bands": 1, "y": YB, "combs": 1}

        def bank(tag):
            return psum.tile([P, W], F32, name="bank_" + tag, tag=tag, bufs=bank_bufs[tag])

        ident = keep.tile([P, P], F32, name="ident")
        floor_rows = keep.tile([P, 2 * P], BF16, name="floor_rows")
        floor_cols = keep.tile([P, 16], F32, name="floor_cols")
        g_plane = keep.tile([P, PASSES, FRAMES], U8, name="g_plane", align_bytes=64)
        y_plane = planes.tile([P, FRAMES], U8, name="y_plane", align_bytes=64)
        warm = keep.tile([P, 8], F32, name="warm")

        g_codes, bands_sb, r_sb, combs_sb = {}, {}, {}, {}
        c_grouped, c_codes, c_scales = {}, {}, {}
        c_bank, b_bank, y_bank, mx_bank, rec_bank = {}, {}, {}, {}, {}
        rs, rec, num, y, y_bf, y_grouped, y_codes = {}, {}, {}, {}, {}, {}, {}

        def place(m):
            bg, fh = divmod(m, HALVES)
            return slice(fh * W, (fh + 1) * W), slice(bg * W, (bg + 1) * W)

        def load_g(fh):
            g_codes[fh] = keep.tile([P, PASSES, W], U32, name="g_codes%d" % fh, align_bytes=64)
            src = g_words[:, :, fh * W : (fh + 1) * W, :].rearrange("g p n t -> p g (n t)")
            nc.sync.dma_start(out=g_codes[fh][:].bitcast(I32), in_=src.bitcast(I32))

        def load_block(src, store, label, fh, bg, count):
            frames = slice(fh * W, (fh + 1) * W)
            block = keep.tile([P, 4, count * W], BF16, name="%s%d%d" % (label, fh, bg))
            cols = src[frames, bg * W : (bg + count) * W]
            nc.sync.dma_start(out=block[:], in_=cols.rearrange("(i p) b -> p i b", p=P))
            for k in range(count):
                store[(bg + k) * HALVES + fh] = (block, k)

        def load_bands(fh, bg, count):
            load_block(bands, bands_sb, "bands", fh, bg, count)

        def load_r(fh, bg, count):
            load_block(r, r_sb, "r", fh, bg, count)

        def load_combs(c):
            combs_sb[c] = keep.tile([P, 2, PITCHES], BF16, name="combs%d" % c)
            rows = combs[c * 256 : (c + 1) * 256, :]
            nc.sync.dma_start(out=combs_sb[c][:], in_=rows.rearrange("(p j) k -> p j k", j=2))

        def turn_combs(c, g, tag):
            c_bank[c, g] = bank(tag)
            words = combs_sb[c][:].bitcast(F32)
            for j in range(2):
                for u in range(2):
                    col = (2 * j + u) * P
                    nc.tensor.transpose(
                        c_bank[c, g][:, col : col + P], words[:, j, 256 * g + u : 256 * (g + 1) : 2], ident[:]
                    )

        def copy_combs(c, g, on_vector):
            bg, h = divmod(c, 2)
            if h == 0:
                c_grouped[2 * bg + g] = work.tile([P, 4 * W], BF16, name="c_grouped", bufs=3, align_bytes=64)
            dst = c_grouped[2 * bg + g][:].bitcast(F32)[:, h * W : (h + 1) * W].rearrange("k (p v) -> k p v", v=4)
            src = c_bank[c, g][:].rearrange("k (v p) -> k p v", v=4)
            if on_vector:
                nc.vector.tensor_copy(out=dst, in_=src)
            else:
                nc.scalar.copy(out=dst, in_=src)

        def quantize_combs(c):
            bg, g = divmod(c, PASSES)
            c_codes[bg, g] = work.tile([P, W], U32, name="c_codes", bufs=4, align_bytes=64)
            c_scales[bg, g] = work.tile([P, W], U8, name="c_scales", bufs=4, align_bytes=64)
            nc.vector.quantize_mx(
                out=c_codes[bg, g][:].bitcast(E4M3), scales=c_scales[bg, g][:], in_=c_grouped[c][:]
            )

        def turn_bands(b, tag):
            m, j = divmod(b, 2)
            b_bank[b] = bank(tag)
            block, k = bands_sb[m]
            words = block[:].bitcast(F32)[:, :, k * 256 : (k + 1) * 256]
            for i in range(4):
                nc.tensor.transpose(b_bank[b][:, i * P : (i + 1) * P], words[:, i, j * P : (j + 1) * P], ident[:])

        def inverse_root(b):
            m, j = divmod(b, 2)
            rs[b] = work.tile([P, 2, W], F32, name="rs", bufs=2)
            src = b_bank[b][:].bitcast(BF16).rearrange("p (f e) -> p e f", e=2)
            for e in range(2):
                col = 2 * (2 * (m // HALVES) + j) + e
                nc.scalar.activation(
                    out=rs[b][:, e, :], in_=src[:, e, :], func=ACT.Abs_reciprocal_sqrt, bias=floor_cols[:, col : col + 1]
                )

        def square(b):
            rec[b] = work.tile([P, 2, W], F32, name="rec", bufs=6)
            if b < V_SQUARES:
                nc.vector.tensor_tensor(out=rec[b][:], in0=rs[b][:], in1=rs[b][:], op=ALU.mult)
            else:
                nc.scalar.activation(out=rec[b][:], in_=rs[b][:], func=ACT.Square)

        def turn_rec(n):
            m, i = divmod(n, 4)
            rec_bank[n] = bank("rec")
            for j in range(2):
                for e in range(2):
                    col = (2 * j + e) * P
                    nc.tensor.transpose(
                        rec_bank[n][:, col : col + P], rec[2 * m + j][:, e, i * P : (i + 1) * P], ident[:]
                    )

        def product(n, g):
            m, i = divmod(n, 4)
            bg, fh = divmod(m, HALVES)
            if g == 0:
                mx_bank[n] = bank("mx")
            f0 = fh * W + i * P
            nc.tensor.matmul_mx(
                out=mx_bank[n][:],
                lhsT=g_codes[fh][:, g, i * P : (i + 1) * P].bitcast(E5M2),
                lhsT_scale=g_plane[:, g, f0 : f0 + P],
                rhs=c_codes[bg, g][:].bitcast(E4M3),
                rhs_scale=c_scales[bg, g][:],
                start=(g == 0),
                stop=(g == PASSES - 1),
            )

        def add_r(n):
            m, i = divmod(n, 4)
            block, k = r_sb[m]
            num[n] = work.tile([P, W], F32, name="num", bufs=3)
            nc.vector.tensor_tensor(out=num[n][:], in0=mx_bank[n][:], in1=block[:, i, k * W : (k + 1) * W], op=ALU.add)

        def divide(n):
            q, i = divmod(n, 2)
            if i == 0:
                y[q] = work.tile([P, 2, W], F32, name="y", bufs=Y_BUFS)
            nc.vector.tensor_tensor(
                out=y[q][:, i, :].rearrange("f (j p e) -> f j p e", j=2, e=2),
                in0=rec_bank[n][:].rearrange("f (j e p) -> f j p e", j=2, e=2),
                in1=num[n][:].rearrange("f (j p e) -> f j p e", j=2, e=2),
                op=ALU.mult,
            )

        def round_y(n):
            q, i = divmod(n, 2)
            y_bf[n] = work.tile([P, W], BF16, name="y_bf", bufs=4)
            dst = y_bf[n][:].rearrange("f (u p e) -> f u p e", u=2, e=2)
            src = y[q][:, i, :].rearrange("f (p u e) -> f u p e", u=2, e=2)
            if S_ROUND_FROM <= n < V_ROUND_FROM:
                nc.scalar.copy(out=dst, in_=src)
            elif G_ROUND and n < V_ROUND_FROM:
                nc.gpsimd.tensor_scalar(out=dst, in0=src, scalar1=1.0, scalar2=0.0, op0=ALU.mult, op1=ALU.add)
            else:
                nc.vector.tensor_copy(out=dst, in_=src)

        def store_y(n0, count):
            frames, bins = place(n0 // 4)
            f0 = frames.start + (n0 % 4) * P
            dst = out_0[f0 : f0 + count * P, bins].rearrange("(i p) b -> p i b", p=P)
            nc.sync.dma_start(out=dst, in_=y[n0 // 2][:, n0 % 2 : n0 % 2 + count, :])

        def turn_y(n0, count, tag):
            y_bank[n0] = bank(tag)
            for i in range(count):
                words = y_bf[n0 + i][:].bitcast(F32)
                for u in range(2):
                    col = (2 * i + u) * P
                    nc.tensor.transpose(y_bank[n0][:, col : col + P], words[:, u * P : (u + 1) * P], ident[:])

        def y_on_vector(q):
            return V_YCOPY > 0 and q % V_YCOPY == 0 and q < Y_UNTIL

        def copy_y(n0, count, on_vector):
            y_grouped[n0] = work.tile([P, count * W], BF16, name="y_grouped", bufs=4, align_bytes=64)
            dst = y_grouped[n0][:].bitcast(F32).rearrange("p (i m u) -> p i m u", i=count, u=2)
            src = y_bank[n0][:, 0 : count * 2 * P].rearrange("p (i u m) -> p i m u", i=count, u=2)
            if on_vector:
                nc.vector.tensor_copy(out=dst, in_=src)
            else:
                nc.scalar.copy(out=dst, in_=src)

        def quantize_y(n0, count):
            m, i = divmod(n0, 4)
            bg, fh = divmod(m, HALVES)
            if i == 0 and fh == 0:
                y_codes[bg] = planes.tile([P, FRAMES], U32, name="y_codes", bufs=2, align_bytes=64)
            f0 = fh * W + i * P
            nc.vector.quantize_mx(
                out=y_codes[bg][:, f0 : f0 + count * P].bitcast(E4M3),
                scales=y_plane[4 * bg : P, f0 : f0 + count * P],
                in_=y_grouped[n0][:],
            )

        def store_codes(n0, count):
            m, i = divmod(n0, 4)
            bg, fh = divmod(m, HALVES)
            f0 = fh * W + i * P
            dst = out_1[bg, :, f0 : f0 + count * P, :].rearrange("p m t -> p (m t)")
            nc.sync.dma_start(out=dst.bitcast(I32), in_=y_codes[bg][:, f0 : f0 + count * P].bitcast(I32))

        def store_scales(queues):
            cols = slice(0, FRAMES)
            for quad in range(4):
                dst = out_2[:, 4 * quad : 4 * quad + 4, cols]
                queues[quad % 2].dma_start(out=dst.bitcast(I32), in_=y_plane[32 * quad : 32 * quad + 16, cols].bitcast(I32))

        nc.vector.memset(floor_rows[:], 0.0)
        make_identity(nc, ident[:])
        nc.vector.memset(warm[:], 1.0)
        nc.scalar.activation(out=warm[:, 4:8], in_=warm[:, 0:4], func=ACT.Abs_reciprocal_sqrt)
        if WARM:
            zeros = keep.tile([P, 4 * W], BF16, name="zeros", align_bytes=64)
            w_codes = keep.tile([P, W + P], U32, name="w_codes", align_bytes=64)
            w_scales = keep.tile([P, W + P], U8, name="w_scales", align_bytes=64)
            nc.vector.memset(zeros[:].bitcast(I32), 0)
        nc.vector.memset(g_plane[:].rearrange("p g n -> p (g n)").bitcast(I32), 0)
        if WARM:
            nc.vector.quantize_mx(out=w_codes[:, W:].bitcast(E5M2), scales=w_scales[:, W:], in_=zeros[:, 0:W])
            nc.vector.quantize_mx(out=w_codes[:, 0:W].bitcast(E4M3), scales=w_scales[:, 0:W], in_=zeros[:])
            warm_bank = bank("mx")

        def warm_up(count):
            for k in range(count if WARM else 0):
                nc.tensor.matmul_mx(
                    out=warm_bank[:], lhsT=w_codes[:, W:].bitcast(E5M2), lhsT_scale=w_scales[:, W:],
                    rhs=w_codes[:, 0:W].bitcast(E4M3), rhs_scale=w_scales[:, 0:W], start=True, stop=True,
                )

        load_bands(0, 0, 1)
        nc.sync.dma_start(out=floor_rows[0:8, :], in_=floor.rearrange("(j w) -> j w", j=8))
        load_combs(0)
        load_combs(1)
        for quad in range(4):
            src = g_scales[:, 4 * quad : 4 * quad + 4, :].rearrange("g r n -> r g n")
            nc.scalar.dma_start(out=g_plane[32 * quad : 32 * quad + 4, :, :].bitcast(I32), in_=src.bitcast(I32))
        load_bands(1, 0, 1)
        load_g(0)
        load_combs(2)
        load_r(0, 0, 1)
        load_combs(3)
        load_bands(0, 1, 1)
        load_g(1)
        load_r(1, 0, 1)
        load_combs(4)
        load_bands(1, 1, 1)
        load_r(0, 1, 1)
        load_combs(5)
        load_bands(0, 2, 2)
        load_r(1, 1, 1)
        load_combs(6)
        load_bands(1, 2, 2)
        load_r(0, 2, 2)
        load_combs(7)
        load_r(1, 2, 2)

        warm_up(W0)
        floor_bank = bank("y")
        nc.tensor.transpose(floor_bank[:, 0:P], floor_rows[:].bitcast(F32), ident[:])
        nc.vector.tensor_copy(out=floor_cols[:], in_=floor_bank[:].bitcast(BF16)[:, 0:16])
        turn_bands(0, "rec")
        warm_up(W1)
        inverse_root(0)
        turn_combs(0, 0, "combs")
        copy_combs(0, 0, True)
        turn_combs(0, 1, "y")
        square(0)
        copy_combs(0, 1, HV1)
        warm_up(W3)
        turn_combs(1, 0, "mx")
        copy_combs(1, 0, True)
        turn_combs(1, 1, "combs")
        copy_combs(1, 1, HV3)
        quantize_combs(0)
        quantize_combs(1)
        turn_bands(1, "rec")
        inverse_root(1)
        turn_bands(2, "bands")
        warm_up(W2)
        if EARLY:
            turn_combs(2, 0, "y")
            copy_combs(2, 0, True)

        def unit(n):
            return 0 <= n < UNITS

        def pair(q):
            return 0 <= q < PAIRS

        combs_jobs = {}
        for bg in range(1, GROUPS):
            for k in range(4):
                if (bg, k) != (1, 0) or not EARLY:
                    combs_jobs.setdefault(max(4 * bg - C_LEAD + k, -1), []).append((2 * bg + k // 2, k % 2))

        for q in range(-1, PAIRS):
            a, b = 2 * q, 2 * q + 1
            jobs = combs_jobs.get(q, [])
            turned = combs_jobs.get(q - 1, [])
            if unit(a + 2):
                for n in ((a + 2, a + 3) if BURST else (a + 2,)):
                    for g in range(PASSES):
                        product(n, g)
            for c, h in jobs[:1]:
                turn_combs(c, h, "combs")
            if unit(b):
                turn_rec(b)
            if pair(q + 2):
                square(q + 2)
            if pair(q + 3):
                inverse_root(q + 3)
            if unit(b):
                add_r(b)
            if unit(a):
                divide(a)
                if q == PAIRS - 1:
                    store_y(a, 1)
            if Q_STEP == 0:
                for c, g in turned:
                    if c % 2 == 1:
                        quantize_combs(c - 1 + g)
            if unit(a - 1):
                round_y(a - 1)
            if pair(q - 2):
                copy_y(a - 4, 2, y_on_vector(q - 2))
            for c, h in jobs[:1]:
                copy_combs(c, h, 2 * c + h < V_CCOPY)
            if unit(b + 2) and not BURST:
                for g in range(PASSES):
                    product(b + 2, g)
            if B_FIRST and pair(q + 4):
                turn_bands(q + 4, "bands")
            if unit(b + 1):
                turn_rec(b + 1)
                add_r(b + 1)
            if not B_FIRST and pair(q + 4):
                turn_bands(q + 4, "bands")
            if unit(b):
                divide(b)
                if q < PAIRS - 1:
                    store_y(a, 2)
            if Q_STEP == 1:
                for c, g in turned:
                    if c % 2 == 1:
                        quantize_combs(c - 1 + g)
            if pair(q - 2) and q < PAIRS - 1:
                quantize_y(a - 4, 2)
                if q % 4 == 1 and q > 1:
                    store_codes(a - 10, 8)
            if unit(a):
                round_y(a)
            if pair(q - 1):
                turn_y(a - 2, 2, "y")
            for c, h in jobs[1:]:
                turn_combs(c, h, "combs")
                copy_combs(c, h, 2 * c + h < V_CCOPY)

        last = UNITS - 1
        store_y(last, 1)
        round_y(last)
        copy_y(last - 3, 2, False)
        turn_y(last - 1, 1, "bands")
        turn_y(last, 1, "combs")
        quantize_y(last - 5, 2)
        store_codes(last - 7, 4)
        copy_y(last - 1, 1, False)
        quantize_y(last - 3, 2)
        store_codes(last - 3, 2)
        copy_y(last, 1, TAILV)
        quantize_y(last - 1, 1)
        quantize_y(last, 1)
        store_codes(last - 1, 2)
        store_scales((nc.scalar, nc.sync))
